import numpy as np
import ml_dtypes


def mxq(x, axis, fmt="e4m3"):
    dtype, down = {"e4m3": (ml_dtypes.float8_e4m3fn, 7), "e5m2": (ml_dtypes.float8_e5m2, 14)}[fmt]
    v = np.moveaxis(np.asarray(x, np.float32).astype(ml_dtypes.bfloat16).astype(np.float64), axis, -1)
    blocks = v.reshape(v.shape[:-1] + (-1, 32))
    amax = np.abs(blocks).max(-1, keepdims=True)
    byte = np.maximum(np.where(amax > 0, np.frexp(amax)[1] - 1 + 127, 0) - down, 1)
    scale = np.exp2(byte - 127.0)
    codes = (blocks / scale).astype(np.float32).astype(dtype).astype(np.float64)
    return np.moveaxis((codes * scale).reshape(v.shape), -1, axis)


WIDE = False


def mx_kscale(k):
    if not WIDE:
        return np.ones(k)
    levels = np.array([10, -10, 5, -5, 0])
    if k % 512:
        return np.exp2(np.random.permutation(np.resize(levels, k // 32))).repeat(32)
    a = np.empty((k // 512, 16))
    for p in range(k // 512):
        a[p, :8] = np.random.permutation(np.resize(levels, 8))
        for g in range(8):
            far = levels[np.abs(levels - a[p, g]) >= 10]
            a[p, g + 8] = far[np.random.randint(len(far))]
    return np.exp2(a.ravel()).repeat(32)


def f64(x):
    return np.asarray(x).astype(np.float64)


def striped(idx):
    return np.tile(idx.reshape(-1, 16).T, (8, 1)).astype(np.uint16)


def unstriped(offs):
    return offs[:16].T.reshape(-1).astype(np.int64)


def relu(v):
    return np.maximum(v, 0.0)


K, T, E, C, N = 2048, 512, 8, 128, 256


def by_expert(wq, xq):
    return np.concatenate([wq[e].T @ xq[:, e * C:(e + 1) * C] for e in range(E)], axis=1)


def setup_inputs():
    n = np.random.standard_normal
    s = mx_kscale(K)[:, None]
    first = np.random.permutation(np.repeat(np.arange(E), T // E))
    second = (first + 1 + np.random.permutation(np.repeat(np.arange(E - 1), -(-T // (E - 1)))[:T])) % E
    while np.bincount(second, minlength=E).max() != T // E:
        load = np.bincount(second, minlength=E); hi, lo = int(load.argmax()), int(load.argmin())
        t = np.flatnonzero((second == hi) & (first != lo))[0]; second[t] = lo
    slot_token = np.empty(E * C, np.int64); pos = np.empty((2, T), np.int64); fill = np.zeros(E, np.int64)
    place = np.stack([np.random.permutation(C) for _ in range(E)])
    for r, deal in enumerate((first, second)):
        for t in np.random.permutation(T):
            e = deal[t]; j = e * C + place[e, fill[e]]; fill[e] += 1; slot_token[j] = t; pos[r, t] = j
    g = np.random.uniform(0.2, 0.8, T)
    return {
        "xT": (n((K, T)) * s).astype(np.float32),
        "w": (n((E, K, N)) / np.sqrt(K) / s[None]).astype(np.float32),
        "b": (0.3 * n((N, E))).astype(np.float32),
        "gate": np.stack([np.tile(g, (N, 1)), np.tile(1.0 - g, (N, 1))]).astype(np.float32),
        "offs": striped(slot_token),
        "pos1": striped(pos[0]),
        "pos2": striped(pos[1]),
    }


def reference(xT, w, b, gate, offs, pos1, pos2):
    idx = unstriped(offs)
    xq = mxq(f64(xT)[:, idx], 0, "e4m3")
    y = by_expert(mxq(f64(w), 1, "e4m3"), xq)
    y = relu(y + np.repeat(f64(b), C, axis=1))
    return f64(gate[0]) * y[:, unstriped(pos1)] + f64(gate[1]) * y[:, unstriped(pos2)]

@@ -1,0 +1,165 @@
+from contextlib import ExitStack
+
+import concourse.mybir as mybir
+
+K, T, E, C, N = 2048, 512, 8, 128, 256
+FLOPS = 2 * E * C * K * N
+
+F32 = mybir.dt.float32
+BF16 = mybir.dt.bfloat16
+U32 = mybir.dt.uint32
+U16 = mybir.dt.uint16
+U8 = mybir.dt.uint8
+FP8X4 = mybir.dt.float8_e4m3fn_x4
+ADD, MAX, MULT = mybir.AluOpType.add, mybir.AluOpType.max, mybir.AluOpType.mult
+RELU = mybir.ActivationFunctionType.Relu
+
+P = 128
+PACK = 4
+PASS = P * PACK
+A = K // PASS
+B = N // P
+HALF = 2
+RING = 10
+PIECE = HALF * PACK * N
+CUTS = ((0, 384), (384, 768), (768, 1024))
+V_COLS = 160
+
+
+def tile_routed_moe_kernel(tc, xT, w, b, gate, offs, pos1, pos2, out):
+    nc = tc.nc
+    with ExitStack() as ctx:
+        lists = ctx.enter_context(tc.tile_pool(name="lists", bufs=1))
+        keep = ctx.enter_context(tc.tile_pool(name="keep", bufs=1))
+        xring = ctx.enter_context(tc.tile_pool(name="xring", bufs=4))
+        xgroup = ctx.enter_context(tc.tile_pool(name="xgroup", bufs=2))
+        ring = ctx.enter_context(tc.tile_pool(name="ring", bufs=RING))
+        group = ctx.enter_context(tc.tile_pool(name="group", bufs=6))
+        ends = ctx.enter_context(tc.tile_pool(name="ends", bufs=2))
+        psum = ctx.enter_context(tc.psum_pool(name="psum", bufs=4))
+
+        offs_sb = lists.tile([P, E * C // 16], U16, name="offs_sb")
+        pos1_sb = lists.tile([P, T // 16], U16, name="pos1_sb")
+        pos2_sb = lists.tile([P, T // 16], U16, name="pos2_sb")
+        bias = keep.tile([P, B, E], F32, name="bias")
+        xq = keep.tile([P, A, T], U32, name="xq", align_bytes=64)
+        xs = keep.tile([P, T], U8, name="xs", align_bytes=64)
+        gq = keep.tile([P, A, E * C], U32, name="gq", align_bytes=64)
+        gs = keep.tile([P, E * C], U8, name="gs", align_bytes=64)
+        wq = keep.tile([P, E * A * N], U32, name="wq", align_bytes=64)
+        ws = keep.tile([P, E * A * N], U8, name="ws", align_bytes=64)
+        y = [keep.tile([P, E * C], F32, name="y%d" % f) for f in range(B)]
+
+        warm = keep.tile([P, 1], F32, name="warm")
+        nc.vector.memset(warm[:], 0.0)
+        nc.scalar.activation(warm[:], warm[:], RELU)
+        nc.gpsimd.memset(xs[:], 0)
+
+        x_rows = xT.rearrange("(a p t) n -> a p (t n)", p=P, t=PACK)
+        x_raw = []
+        for a in range(A):
+            raw = xring.tile([P, PACK * T], F32, name="x_raw")
+            nc.sync.dma_start(raw[:], x_rows[a])
+            x_raw.append(raw)
+            if a == 0:
+                nc.sync.dma_start(offs_sb[:], offs)
+        nc.sync.dma_start(bias[:], b.rearrange("(f p) e -> p f e", p=P))
+        nc.sync.dma_start(pos1_sb[:], pos1)
+        nc.sync.dma_start(pos2_sb[:], pos2)
+
+        pieces = [(e, h) for e in range(E) for h in range(A // HALF)]
+        w_raw = []
+
+        def load(m):
+            e, h = pieces[m]
+            raw = ring.tile([P, PIECE], F32, name="w_raw", tag="raw")
+            rows = w[e].rearrange("(a p t) n -> p a (t n)", p=P, t=PACK)
+            view = raw[:].rearrange("p (a f) -> p a f", a=HALF)
+            if e < E - 1:
+                nc.sync.dma_start(view, rows[:, HALF * h : HALF * (h + 1), :])
+            else:
+                for i in range(HALF):
+                    nc.sync.dma_start(view[:, i, :], rows[:, HALF * h + i, :])
+            w_raw.append(raw)
+
+        for m in range(RING):
+            load(m)
+
+        for a in range(A):
+            grouped = xgroup.tile([P, T * PACK], BF16, name="x_grouped", align_bytes=64)
+            nc.scalar.copy(
+                grouped[:].rearrange("p (c i t) -> p c t i", t=PACK, i=4),
+                x_raw[a][:].rearrange("p (t c i) -> p c t i", t=PACK, i=4),
+            )
+            nc.vector.quantize_mx(out=xq[:, a, :].bitcast(FP8X4), scales=xs[4 * a : P, :], in_=grouped[:])
+            for lo, hi in CUTS:
+                nc.vector.tensor_copy(gq[:, a, lo:hi], xq[:, a, :].indirect(offs_sb[:, lo // 16 : hi // 16]))
+        for lo, hi in CUTS:
+            nc.vector.tensor_copy(gs[:, lo:hi], xs[:].indirect(offs_sb[:, lo // 16 : hi // 16]))
+
+        def interleave(engine, grouped, raw, lo, hi):
+            dst = grouped[:].rearrange("p (a c i t) -> p a c t i", a=HALF, t=PACK, i=4)[:, :, lo // 4 : hi // 4]
+            src = raw[:].rearrange("p (a t c i) -> p a c t i", a=HALF, t=PACK, i=4)[:, :, lo // 4 : hi // 4]
+            engine(dst, src)
+
+        def interleave_pass(engine, grouped, raw, i, lo, hi):
+            dst = grouped[:].rearrange("p (a c i t) -> p a c t i", a=HALF, t=PACK, i=4)[:, i, lo // 4 : hi // 4]
+            src = raw[:].rearrange("p (a t c i) -> p a c t i", a=HALF, t=PACK, i=4)[:, i, lo // 4 : hi // 4]
+            engine(dst, src)
+
+        gate_raw = None
+        for e in range(E):
+            last = e == E - 1
+            for h in range(A // HALF):
+                m = e * (A // HALF) + h
+                grouped = group.tile([P, PIECE], BF16, name="w_grouped", align_bytes=64)
+                raw = w_raw[m]
+                base = e * A * N + h * HALF * N
+                if last:
+                    for i in range(HALF):
+                        interleave_pass(nc.vector.tensor_copy, grouped, raw, i, 0, V_COLS)
+                        interleave_pass(nc.scalar.copy, grouped, raw, i, V_COLS, N)
+                        words = slice(base + i * N, base + (i + 1) * N)
+                        nc.vector.quantize_mx(
+                            out=wq[:, words].bitcast(FP8X4), scales=ws[:, words],
+                            in_=grouped[:, i * N * PACK : (i + 1) * N * PACK],
+                        )
+                else:
+                    interleave(nc.scalar.copy if h == 0 else nc.vector.tensor_copy, grouped, raw, 0, N)
+                    words = slice(base, base + HALF * N)
+                    nc.vector.quantize_mx(out=wq[:, words].bitcast(FP8X4), scales=ws[:, words], in_=grouped[:])
+                if m + RING < len(pieces):
+                    load(m + RING)
+                elif m + RING == len(pieces):
+                    gate_raw = ring.tile([P, B, 2, T], F32, name="gate_raw", tag="raw")
+                    for f in range(B):
+                        nc.sync.dma_start(gate_raw[:, f], gate[:, f * P : (f + 1) * P, :].rearrange("r p n -> p r n"))
+
+            acc = [psum.tile([P, C], F32, name="acc%d" % f) for f in range(B)]
+            slots = slice(e * C, (e + 1) * C)
+            for a in range(A):
+                for f in range(B):
+                    words = slice(e * A * N + a * N + f * P, e * A * N + a * N + (f + 1) * P)
+                    nc.tensor.matmul_mx(
+                        out=acc[f][:],
+                        lhsT=wq[:, words].bitcast(FP8X4),
+                        lhsT_scale=ws[:, words],
+                        rhs=gq[:, a, slots].bitcast(FP8X4),
+                        rhs_scale=gs[4 * a : P, slots],
+                        start=(a == 0),
+                        stop=(a == A - 1),
+                    )
+            for f in range(B):
+                if last and f == B - 1:
+                    nc.vector.tensor_scalar(y[f][:, slots], acc[f][:], bias[:, f, e : e + 1], 0.0, ADD, MAX)
+                else:
+                    nc.scalar.activation(y[f][:, slots], acc[f][:], RELU, bias=bias[:, f, e : e + 1])
+
+        for f in range(B):
+            first = ends.tile([P, T], F32, name="first")
+            second = ends.tile([P, T], F32, name="second")
+            total = ends.tile([P, T], F32, name="total")
+            nc.vector.tensor_tensor(first[:], y[f][:].indirect(pos1_sb[:]), gate_raw[:, f, 0, :], MULT)
+            nc.vector.tensor_tensor(second[:], y[f][:].indirect(pos2_sb[:]), gate_raw[:, f, 1, :], MULT)
+            nc.vector.tensor_add(total[:], first[:], second[:])
+            nc.sync.dma_start(out[f * P : (f + 1) * P, :], total[:])

@@ -11,7 +11,7 @@ U32 = mybir.dt.uint32
 U16 = mybir.dt.uint16
 U8 = mybir.dt.uint8
 FP8X4 = mybir.dt.float8_e4m3fn_x4
-ADD, MAX, MULT = mybir.AluOpType.add, mybir.AluOpType.max, mybir.AluOpType.mult
+MULT = mybir.AluOpType.mult
 RELU = mybir.ActivationFunctionType.Relu
 
 P = 128
@@ -24,6 +24,7 @@ RING = 10
 PIECE = HALF * PACK * N
 CUTS = ((0, 384), (384, 768), (768, 1024))
 V_COLS = 160
+V_HALF = 80
 
 
 def tile_routed_moe_kernel(tc, xT, w, b, gate, offs, pos1, pos2, out):
@@ -64,8 +65,6 @@ def tile_routed_moe_kernel(tc, xT, w, b, gate, offs, pos1, pos2, out):
             if a == 0:
                 nc.sync.dma_start(offs_sb[:], offs)
         nc.sync.dma_start(bias[:], b.rearrange("(f p) e -> p f e", p=P))
-        nc.sync.dma_start(pos1_sb[:], pos1)
-        nc.sync.dma_start(pos2_sb[:], pos2)
 
         pieces = [(e, h) for e in range(E) for h in range(A // HALF)]
         w_raw = []
@@ -75,12 +74,17 @@ def tile_routed_moe_kernel(tc, xT, w, b, gate, offs, pos1, pos2, out):
             raw = ring.tile([P, PIECE], F32, name="w_raw", tag="raw")
             rows = w[e].rearrange("(a p t) n -> p a (t n)", p=P, t=PACK)
             view = raw[:].rearrange("p (a f) -> p a f", a=HALF)
-            if e < E - 1:
+            w_raw.append(raw)
+            if m < len(pieces) - 1:
                 nc.sync.dma_start(view, rows[:, HALF * h : HALF * (h + 1), :])
             else:
-                for i in range(HALF):
-                    nc.sync.dma_start(view[:, i, :], rows[:, HALF * h + i, :])
-            w_raw.append(raw)
+                halves = raw[:].rearrange("p (f i t n) -> p f i t n", f=B, i=HALF, t=PACK)
+                cols = w[e].rearrange("(a p t) n -> p a t n", p=P, t=PACK)
+                for f in range(B):
+                    for i in range(HALF):
+                        nc.sync.dma_start(halves[:, f, i], cols[:, HALF * h + i, :, f * P : (f + 1) * P])
+                nc.sync.dma_start(pos1_sb[:], pos1)
+                nc.sync.dma_start(pos2_sb[:], pos2)
 
         for m in range(RING):
             load(m)
@@ -98,68 +102,76 @@ def tile_routed_moe_kernel(tc, xT, w, b, gate, offs, pos1, pos2, out):
             nc.vector.tensor_copy(gs[:, lo:hi], xs[:].indirect(offs_sb[:, lo // 16 : hi // 16]))
 
         def interleave(engine, grouped, raw, lo, hi):
-            dst = grouped[:].rearrange("p (a c i t) -> p a c t i", a=HALF, t=PACK, i=4)[:, :, lo // 4 : hi // 4]
-            src = raw[:].rearrange("p (a t c i) -> p a c t i", a=HALF, t=PACK, i=4)[:, :, lo // 4 : hi // 4]
+            dst = grouped.rearrange("p (a c i t) -> p a c t i", a=HALF, t=PACK, i=4)[:, :, lo // 4 : hi // 4]
+            src = raw.rearrange("p (a t c i) -> p a c t i", a=HALF, t=PACK, i=4)[:, :, lo // 4 : hi // 4]
             engine(dst, src)
 
-        def interleave_pass(engine, grouped, raw, i, lo, hi):
-            dst = grouped[:].rearrange("p (a c i t) -> p a c t i", a=HALF, t=PACK, i=4)[:, i, lo // 4 : hi // 4]
-            src = raw[:].rearrange("p (a t c i) -> p a c t i", a=HALF, t=PACK, i=4)[:, i, lo // 4 : hi // 4]
-            engine(dst, src)
+        def multiply(acc, e, a, f, first_word):
+            words, slots = slice(first_word, first_word + P), slice(e * C, (e + 1) * C)
+            nc.tensor.matmul_mx(
+                out=acc[f][:],
+                lhsT=wq[:, words].bitcast(FP8X4),
+                lhsT_scale=ws[:, words],
+                rhs=gq[:, a, slots].bitcast(FP8X4),
+                rhs_scale=gs[4 * a : P, slots],
+                start=(a == 0),
+                stop=(a == A - 1),
+            )
 
-        gate_raw = None
-        for e in range(E):
-            last = e == E - 1
-            for h in range(A // HALF):
-                m = e * (A // HALF) + h
-                grouped = group.tile([P, PIECE], BF16, name="w_grouped", align_bytes=64)
-                raw = w_raw[m]
-                base = e * A * N + h * HALF * N
-                if last:
-                    for i in range(HALF):
-                        interleave_pass(nc.vector.tensor_copy, grouped, raw, i, 0, V_COLS)
-                        interleave_pass(nc.scalar.copy, grouped, raw, i, V_COLS, N)
-                        words = slice(base + i * N, base + (i + 1) * N)
-                        nc.vector.quantize_mx(
-                            out=wq[:, words].bitcast(FP8X4), scales=ws[:, words],
-                            in_=grouped[:, i * N * PACK : (i + 1) * N * PACK],
-                        )
-                else:
-                    interleave(nc.scalar.copy if h == 0 else nc.vector.tensor_copy, grouped, raw, 0, N)
-                    words = slice(base, base + HALF * N)
-                    nc.vector.quantize_mx(out=wq[:, words].bitcast(FP8X4), scales=ws[:, words], in_=grouped[:])
-                if m + RING < len(pieces):
-                    load(m + RING)
-                elif m + RING == len(pieces):
-                    gate_raw = ring.tile([P, B, 2, T], F32, name="gate_raw", tag="raw")
-                    for f in range(B):
-                        nc.sync.dma_start(gate_raw[:, f], gate[:, f * P : (f + 1) * P, :].rearrange("r p n -> p r n"))
+        def quantize(first_word, grouped, count):
+            words = slice(first_word, first_word + count)
+            nc.vector.quantize_mx(out=wq[:, words].bitcast(FP8X4), scales=ws[:, words], in_=grouped)
 
-            acc = [psum.tile([P, C], F32, name="acc%d" % f) for f in range(B)]
-            slots = slice(e * C, (e + 1) * C)
-            for a in range(A):
+        def finish(acc, e, f):
+            nc.scalar.activation(y[f][:, e * C : (e + 1) * C], acc[f][:], RELU, bias=bias[:, f, e : e + 1])
+
+        acc, gate_raw = None, None
+        for m, (e, h) in enumerate(pieces):
+            if h == 0:
+                acc = [psum.tile([P, C], F32, name="acc%d" % f) for f in range(B)]
+            grouped = group.tile([P, PIECE], BF16, name="w_grouped", align_bytes=64)
+            raw = w_raw[m]
+            base = m * HALF * N
+            if m == len(pieces) - 1:
                 for f in range(B):
-                    words = slice(e * A * N + a * N + f * P, e * A * N + a * N + (f + 1) * P)
-                    nc.tensor.matmul_mx(
-                        out=acc[f][:],
-                        lhsT=wq[:, words].bitcast(FP8X4),
-                        lhsT_scale=ws[:, words],
-                        rhs=gq[:, a, slots].bitcast(FP8X4),
-                        rhs_scale=gs[4 * a : P, slots],
-                        start=(a == 0),
-                        stop=(a == A - 1),
-                    )
-            for f in range(B):
-                if last and f == B - 1:
-                    nc.vector.tensor_scalar(y[f][:, slots], acc[f][:], bias[:, f, e : e + 1], 0.0, ADD, MAX)
-                else:
-                    nc.scalar.activation(y[f][:, slots], acc[f][:], RELU, bias=bias[:, f, e : e + 1])
+                    part = slice(f * PIECE // B, (f + 1) * PIECE // B)
+                    v_cols = V_HALF if f == 0 else 0
+                    if v_cols > 0:
+                        interleave(nc.vector.tensor_copy, grouped[:, part], raw[:, part], 0, v_cols)
+                    interleave(nc.scalar.copy, grouped[:, part], raw[:, part], v_cols, P)
+                    quantize(base + f * HALF * P, grouped[:, part], HALF * P)
+                    for i in range(HALF):
+                        multiply(acc, e, HALF * h + i, f, base + (f * HALF + i) * P)
+                    finish(acc, e, f)
+                continue
+            v_cols = V_COLS if e == E - 1 else (0, N)[h]
+            if v_cols > 0:
+                interleave(nc.vector.tensor_copy, grouped[:], raw[:], 0, v_cols)
+            if v_cols < N:
+                interleave(nc.scalar.copy, grouped[:], raw[:], v_cols, N)
+            quantize(base, grouped[:], HALF * N)
+            if m + RING < len(pieces):
+                load(m + RING)
+            elif m + RING == len(pieces):
+                gate_raw = ring.tile([P, B, 2, T], F32, name="gate_raw", tag="raw")
+                for f in range(B):
+                    nc.sync.dma_start(gate_raw[:, f], gate[:, f * P : (f + 1) * P, :].rearrange("r p n -> p r n"))
+            for i in range(HALF):
+                for f in range(B):
+                    multiply(acc, e, HALF * h + i, f, base + i * N + f * P)
+            if h == 1:
+                for f in range(B):
+                    finish(acc, e, f)
 
         for f in range(B):
             first = ends.tile([P, T], F32, name="first")
             second = ends.tile([P, T], F32, name="second")
             total = ends.tile([P, T], F32, name="total")
             nc.vector.tensor_tensor(first[:], y[f][:].indirect(pos1_sb[:]), gate_raw[:, f, 0, :], MULT)
-            nc.vector.tensor_tensor(second[:], y[f][:].indirect(pos2_sb[:]), gate_raw[:, f, 1, :], MULT)
-            nc.vector.tensor_add(total[:], first[:], second[:])
-            nc.sync.dma_start(out[f * P : (f + 1) * P, :], total[:])
+            parts = f + 1
+            for lo in range(0, T, T // parts):
+                cut = slice(lo, lo + T // parts)
+                offsets = pos2_sb[:, cut.start // 16 : cut.stop // 16]
+                nc.vector.tensor_tensor(second[:, cut], y[f][:].indirect(offsets), gate_raw[:, f, 1, cut], MULT)
+                nc.vector.tensor_add(total[:, cut], first[:, cut], second[:, cut])
+                nc.sync.dma_start(out[f * P : (f + 1) * P, cut], total[:, cut])

@@ -24,7 +24,7 @@ RING = 10
 PIECE = HALF * PACK * N
 CUTS = ((0, 384), (384, 768), (768, 1024))
 V_COLS = 160
-V_HALF = 80
+V_LAST = 176
 
 
 def tile_routed_moe_kernel(tc, xT, w, b, gate, offs, pos1, pos2, out):
@@ -36,7 +36,7 @@ def tile_routed_moe_kernel(tc, xT, w, b, gate, offs, pos1, pos2, out):
         xgroup = ctx.enter_context(tc.tile_pool(name="xgroup", bufs=2))
         ring = ctx.enter_context(tc.tile_pool(name="ring", bufs=RING))
         group = ctx.enter_context(tc.tile_pool(name="group", bufs=6))
-        ends = ctx.enter_context(tc.tile_pool(name="ends", bufs=2))
+        ends = ctx.enter_context(tc.tile_pool(name="ends", bufs=1))
         psum = ctx.enter_context(tc.psum_pool(name="psum", bufs=4))
 
         offs_sb = lists.tile([P, E * C // 16], U16, name="offs_sb")
@@ -78,11 +78,8 @@ def tile_routed_moe_kernel(tc, xT, w, b, gate, offs, pos1, pos2, out):
             if m < len(pieces) - 1:
                 nc.sync.dma_start(view, rows[:, HALF * h : HALF * (h + 1), :])
             else:
-                halves = raw[:].rearrange("p (f i t n) -> p f i t n", f=B, i=HALF, t=PACK)
-                cols = w[e].rearrange("(a p t) n -> p a t n", p=P, t=PACK)
-                for f in range(B):
-                    for i in range(HALF):
-                        nc.sync.dma_start(halves[:, f, i], cols[:, HALF * h + i, :, f * P : (f + 1) * P])
+                for i in range(HALF):
+                    nc.sync.dma_start(view[:, i], rows[:, HALF * h + i])
                 nc.sync.dma_start(pos1_sb[:], pos1)
                 nc.sync.dma_start(pos2_sb[:], pos2)
 
@@ -133,15 +130,21 @@ def tile_routed_moe_kernel(tc, xT, w, b, gate, offs, pos1, pos2, out):
             raw = w_raw[m]
             base = m * HALF * N
             if m == len(pieces) - 1:
+                for i in range(HALF):
+                    part = slice(i * N * PACK, (i + 1) * N * PACK)
+                    dst = grouped[:, part].rearrange("p (c q t) -> p c t q", t=PACK, q=4)
+                    src = raw[:, part].rearrange("p (t c q) -> p c t q", t=PACK, q=4)
+                    cut = V_LAST // 4
+                    nc.vector.tensor_copy(dst[:, :cut], src[:, :cut])
+                    nc.scalar.copy(dst[:, cut:], src[:, cut:])
+                    if i == 0:
+                        quantize(base, grouped[:, part], N)
+                    for f in range(B):
+                        if i > 0:
+                            own = slice(part.start + f * P * PACK, part.start + (f + 1) * P * PACK)
+                            quantize(base + i * N + f * P, grouped[:, own], P)
+                        multiply(acc, e, HALF * h + i, f, base + i * N + f * P)
                 for f in range(B):
-                    part = slice(f * PIECE // B, (f + 1) * PIECE // B)
-                    v_cols = V_HALF if f == 0 else 0
-                    if v_cols > 0:
-                        interleave(nc.vector.tensor_copy, grouped[:, part], raw[:, part], 0, v_cols)
-                    interleave(nc.scalar.copy, grouped[:, part], raw[:, part], v_cols, P)
-                    quantize(base + f * HALF * P, grouped[:, part], HALF * P)
-                    for i in range(HALF):
-                        multiply(acc, e, HALF * h + i, f, base + (f * HALF + i) * P)
                     finish(acc, e, f)
                 continue
             v_cols = V_COLS if e == E - 1 else (0, N)[h]
@@ -163,15 +166,24 @@ def tile_routed_moe_kernel(tc, xT, w, b, gate, offs, pos1, pos2, out):
                 for f in range(B):
                     finish(acc, e, f)
 
-        for f in range(B):
-            first = ends.tile([P, T], F32, name="first")
-            second = ends.tile([P, T], F32, name="second")
-            total = ends.tile([P, T], F32, name="total")
-            nc.vector.tensor_tensor(first[:], y[f][:].indirect(pos1_sb[:]), gate_raw[:, f, 0, :], MULT)
-            parts = f + 1
-            for lo in range(0, T, T // parts):
-                cut = slice(lo, lo + T // parts)
-                offsets = pos2_sb[:, cut.start // 16 : cut.stop // 16]
-                nc.vector.tensor_tensor(second[:, cut], y[f][:].indirect(offsets), gate_raw[:, f, 1, cut], MULT)
-                nc.vector.tensor_add(total[:, cut], first[:, cut], second[:, cut])
-                nc.sync.dma_start(out[f * P : (f + 1) * P, cut], total[:, cut])
+        first = [ends.tile([P, T], F32, name="first%d" % f) for f in range(B)]
+        second = [ends.tile([P, T], F32, name="second%d" % f) for f in range(B)]
+        total = [ends.tile([P, T], F32, name="total%d" % f) for f in range(B)]
+
+        def fetch(product, f, pos_sb, r, cut):
+            offsets = pos_sb[:, cut.start // 16 : cut.stop // 16]
+            nc.vector.tensor_tensor(product[f][:, cut], y[f][:].indirect(offsets), gate_raw[:, f, r, cut], MULT)
+
+        def add_and_store(f, cut):
+            nc.vector.tensor_add(total[f][:, cut], first[f][:, cut], second[f][:, cut])
+            nc.sync.dma_start(out[f * P : (f + 1) * P, cut], total[f][:, cut])
+
+        whole, halves = slice(0, T), (slice(0, T // 2), slice(T // 2, T))
+        fetch(first, 0, pos1_sb, 0, whole)
+        fetch(second, 0, pos2_sb, 1, whole)
+        fetch(first, 1, pos1_sb, 0, whole)
+        add_and_store(0, whole)
+        for cut in halves:
+            fetch(second, 1, pos2_sb, 1, cut)
+        for cut in halves:
+            add_and_store(1, cut)

from contextlib import ExitStack

import concourse.mybir as mybir

K, T, E, C, N = 2048, 512, 8, 128, 256
FLOPS = 2 * E * C * K * N

F32 = mybir.dt.float32
BF16 = mybir.dt.bfloat16
U32 = mybir.dt.uint32
U16 = mybir.dt.uint16
U8 = mybir.dt.uint8
FP8X4 = mybir.dt.float8_e4m3fn_x4
MULT = mybir.AluOpType.mult
RELU = mybir.ActivationFunctionType.Relu

P = 128
PACK = 4
PASS = P * PACK
A = K // PASS
B = N // P
HALF = 2
RING = 10
PIECE = HALF * PACK * N
CUTS = ((0, 384), (384, 768), (768, 1024))
V_COLS = 160
V_LAST = 176


def tile_routed_moe_kernel(tc, xT, w, b, gate, offs, pos1, pos2, out):
    nc = tc.nc
    with ExitStack() as ctx:
        lists = ctx.enter_context(tc.tile_pool(name="lists", bufs=1))
        keep = ctx.enter_context(tc.tile_pool(name="keep", bufs=1))
        xring = ctx.enter_context(tc.tile_pool(name="xring", bufs=4))
        xgroup = ctx.enter_context(tc.tile_pool(name="xgroup", bufs=2))
        ring = ctx.enter_context(tc.tile_pool(name="ring", bufs=RING))
        group = ctx.enter_context(tc.tile_pool(name="group", bufs=6))
        ends = ctx.enter_context(tc.tile_pool(name="ends", bufs=1))
        psum = ctx.enter_context(tc.psum_pool(name="psum", bufs=4))

        offs_sb = lists.tile([P, E * C // 16], U16, name="offs_sb")
        pos1_sb = lists.tile([P, T // 16], U16, name="pos1_sb")
        pos2_sb = lists.tile([P, T // 16], U16, name="pos2_sb")
        bias = keep.tile([P, B, E], F32, name="bias")
        xq = keep.tile([P, A, T], U32, name="xq", align_bytes=64)
        xs = keep.tile([P, T], U8, name="xs", align_bytes=64)
        gq = keep.tile([P, A, E * C], U32, name="gq", align_bytes=64)
        gs = keep.tile([P, E * C], U8, name="gs", align_bytes=64)
        wq = keep.tile([P, E * A * N], U32, name="wq", align_bytes=64)
        ws = keep.tile([P, E * A * N], U8, name="ws", align_bytes=64)
        y = [keep.tile([P, E * C], F32, name="y%d" % f) for f in range(B)]

        warm = keep.tile([P, 1], F32, name="warm")
        nc.vector.memset(warm[:], 0.0)
        nc.scalar.activation(warm[:], warm[:], RELU)
        nc.gpsimd.memset(xs[:], 0)

        x_rows = xT.rearrange("(a p t) n -> a p (t n)", p=P, t=PACK)
        x_raw = []
        for a in range(A):
            raw = xring.tile([P, PACK * T], F32, name="x_raw")
            nc.sync.dma_start(raw[:], x_rows[a])
            x_raw.append(raw)
            if a == 0:
                nc.sync.dma_start(offs_sb[:], offs)
        nc.sync.dma_start(bias[:], b.rearrange("(f p) e -> p f e", p=P))

        pieces = [(e, h) for e in range(E) for h in range(A // HALF)]
        w_raw = []

        def load(m):
            e, h = pieces[m]
            raw = ring.tile([P, PIECE], F32, name="w_raw", tag="raw")
            rows = w[e].rearrange("(a p t) n -> p a (t n)", p=P, t=PACK)
            view = raw[:].rearrange("p (a f) -> p a f", a=HALF)
            w_raw.append(raw)
            if m < len(pieces) - 1:
                nc.sync.dma_start(view, rows[:, HALF * h : HALF * (h + 1), :])
            else:
                for i in range(HALF):
                    nc.sync.dma_start(view[:, i], rows[:, HALF * h + i])
                nc.sync.dma_start(pos1_sb[:], pos1)
                nc.sync.dma_start(pos2_sb[:], pos2)

        for m in range(RING):
            load(m)

        for a in range(A):
            grouped = xgroup.tile([P, T * PACK], BF16, name="x_grouped", align_bytes=64)
            nc.scalar.copy(
                grouped[:].rearrange("p (c i t) -> p c t i", t=PACK, i=4),
                x_raw[a][:].rearrange("p (t c i) -> p c t i", t=PACK, i=4),
            )
            nc.vector.quantize_mx(out=xq[:, a, :].bitcast(FP8X4), scales=xs[4 * a : P, :], in_=grouped[:])
            for lo, hi in CUTS:
                nc.vector.tensor_copy(gq[:, a, lo:hi], xq[:, a, :].indirect(offs_sb[:, lo // 16 : hi // 16]))
        for lo, hi in CUTS:
            nc.vector.tensor_copy(gs[:, lo:hi], xs[:].indirect(offs_sb[:, lo // 16 : hi // 16]))

        def interleave(engine, grouped, raw, lo, hi):
            dst = grouped.rearrange("p (a c i t) -> p a c t i", a=HALF, t=PACK, i=4)[:, :, lo // 4 : hi // 4]
            src = raw.rearrange("p (a t c i) -> p a c t i", a=HALF, t=PACK, i=4)[:, :, lo // 4 : hi // 4]
            engine(dst, src)

        def multiply(acc, e, a, f, first_word):
            words, slots = slice(first_word, first_word + P), slice(e * C, (e + 1) * C)
            nc.tensor.matmul_mx(
                out=acc[f][:],
                lhsT=wq[:, words].bitcast(FP8X4),
                lhsT_scale=ws[:, words],
                rhs=gq[:, a, slots].bitcast(FP8X4),
                rhs_scale=gs[4 * a : P, slots],
                start=(a == 0),
                stop=(a == A - 1),
            )

        def quantize(first_word, grouped, count):
            words = slice(first_word, first_word + count)
            nc.vector.quantize_mx(out=wq[:, words].bitcast(FP8X4), scales=ws[:, words], in_=grouped)

        def finish(acc, e, f):
            nc.scalar.activation(y[f][:, e * C : (e + 1) * C], acc[f][:], RELU, bias=bias[:, f, e : e + 1])

        acc, gate_raw = None, None
        for m, (e, h) in enumerate(pieces):
            if h == 0:
                acc = [psum.tile([P, C], F32, name="acc%d" % f) for f in range(B)]
            grouped = group.tile([P, PIECE], BF16, name="w_grouped", align_bytes=64)
            raw = w_raw[m]
            base = m * HALF * N
            if m == len(pieces) - 1:
                for i in range(HALF):
                    part = slice(i * N * PACK, (i + 1) * N * PACK)
                    dst = grouped[:, part].rearrange("p (c q t) -> p c t q", t=PACK, q=4)
                    src = raw[:, part].rearrange("p (t c q) -> p c t q", t=PACK, q=4)
                    cut = V_LAST // 4
                    nc.vector.tensor_copy(dst[:, :cut], src[:, :cut])
                    nc.scalar.copy(dst[:, cut:], src[:, cut:])
                    if i == 0:
                        quantize(base, grouped[:, part], N)
                    for f in range(B):
                        if i > 0:
                            own = slice(part.start + f * P * PACK, part.start + (f + 1) * P * PACK)
                            quantize(base + i * N + f * P, grouped[:, own], P)
                        multiply(acc, e, HALF * h + i, f, base + i * N + f * P)
                for f in range(B):
                    finish(acc, e, f)
                continue
            v_cols = V_COLS if e == E - 1 else (0, N)[h]
            if v_cols > 0:
                interleave(nc.vector.tensor_copy, grouped[:], raw[:], 0, v_cols)
            if v_cols < N:
                interleave(nc.scalar.copy, grouped[:], raw[:], v_cols, N)
            quantize(base, grouped[:], HALF * N)
            if m + RING < len(pieces):
                load(m + RING)
            elif m + RING == len(pieces):
                gate_raw = ring.tile([P, B, 2, T], F32, name="gate_raw", tag="raw")
                for f in range(B):
                    nc.sync.dma_start(gate_raw[:, f], gate[:, f * P : (f + 1) * P, :].rearrange("r p n -> p r n"))
            for i in range(HALF):
                for f in range(B):
                    multiply(acc, e, HALF * h + i, f, base + i * N + f * P)
            if h == 1:
                for f in range(B):
                    finish(acc, e, f)

        first = [ends.tile([P, T], F32, name="first%d" % f) for f in range(B)]
        second = [ends.tile([P, T], F32, name="second%d" % f) for f in range(B)]
        total = [ends.tile([P, T], F32, name="total%d" % f) for f in range(B)]

        def fetch(product, f, pos_sb, r, cut):
            offsets = pos_sb[:, cut.start // 16 : cut.stop // 16]
            nc.vector.tensor_tensor(product[f][:, cut], y[f][:].indirect(offsets), gate_raw[:, f, r, cut], MULT)

        def add_and_store(f, cut):
            nc.vector.tensor_add(total[f][:, cut], first[f][:, cut], second[f][:, cut])
            nc.sync.dma_start(out[f * P : (f + 1) * P, cut], total[f][:, cut])

        whole, halves = slice(0, T), (slice(0, T // 2), slice(T // 2, T))
        fetch(first, 0, pos1_sb, 0, whole)
        fetch(second, 0, pos2_sb, 1, whole)
        fetch(first, 1, pos1_sb, 0, whole)
        add_and_store(0, whole)
        for cut in halves:
            fetch(second, 1, pos2_sb, 1, cut)
        for cut in halves:
            add_and_store(1, cut)
